import numpy as np
import ml_dtypes


def mxq(x, axis, fmt="e4m3"):
    dtype, down = {"e4m3": (ml_dtypes.float8_e4m3fn, 7), "e5m2": (ml_dtypes.float8_e5m2, 14)}[fmt]
    v = np.moveaxis(np.asarray(x, np.float32).astype(ml_dtypes.bfloat16).astype(np.float64), axis, -1)
    blocks = v.reshape(v.shape[:-1] + (-1, 32))
    amax = np.abs(blocks).max(-1, keepdims=True)
    byte = np.maximum(np.where(amax > 0, np.frexp(amax)[1] - 1 + 127, 0) - down, 1)
    scale = np.exp2(byte - 127.0)
    codes = (blocks / scale).astype(np.float32).astype(dtype).astype(np.float64)
    return np.moveaxis((codes * scale).reshape(v.shape), -1, axis)


WIDE = False


def mx_kscale(k):
    if not WIDE:
        return np.ones(k)
    levels = np.array([10, -10, 5, -5, 0])
    if k % 512:
        return np.exp2(np.random.permutation(np.resize(levels, k // 32))).repeat(32)
    a = np.empty((k // 512, 16))
    for p in range(k // 512):
        a[p, :8] = np.random.permutation(np.resize(levels, 8))
        for g in range(8):
            far = levels[np.abs(levels - a[p, g]) >= 10]
            a[p, g + 8] = far[np.random.randint(len(far))]
    return np.exp2(a.ravel()).repeat(32)


def f64(x):
    return np.asarray(x).astype(np.float64)


def striped(idx):
    return np.tile(idx.reshape(-1, 16).T, (8, 1)).astype(np.uint16)


def unstriped(offs):
    return offs[:16].T.reshape(-1).astype(np.int64)


def striped8(idx):
    return np.concatenate([x.reshape(-1, 16).T for x in idx]).astype(np.uint16)


def runs(offs, k):
    lists = np.stack([offs[16 * r : 16 * r + 16].T.reshape(-1) for r in range(8)]).astype(np.int64)
    return lists[np.arange(k) % 512 // 64]


def pack_weight(w):
    k, n = w.shape
    w = f64(np.asarray(w, np.float32).astype(ml_dtypes.bfloat16)).reshape(k // 32, 32, n)
    amax = np.abs(w).max(1)
    byte = np.clip(np.where(amax > 0, np.frexp(amax)[1] - 1 + 127 - 7, 1), 1, 254)
    scaled = (w * np.exp2(127.0 - byte)[:, None, :]).reshape(k, n).astype(np.float32)
    words = np.ascontiguousarray(scaled.reshape(k // 512, 128, 4, n).transpose(0, 1, 3, 2)).astype(ml_dtypes.float8_e4m3fn).view(np.uint8)
    return words, np.ascontiguousarray(byte.astype(np.uint8).reshape(k // 512, 16, n))


def unpack_weight(words, scales):
    g, p, n, _ = words.shape
    vals = np.ascontiguousarray(words).view(ml_dtypes.float8_e4m3fn).astype(np.float64) * np.repeat(np.exp2(scales.astype(np.float64) - 127.0), 8, axis=1)[..., None]
    return vals.transpose(0, 1, 3, 2).reshape(g * 512, n)

def planes(y):
    n, m = y.shape
    v = y.astype(np.float32).astype(ml_dtypes.bfloat16).astype(np.float64).reshape(n // 32, 32, m)
    top = np.abs(v).max(1)
    byte = np.clip(np.where(top > 0, np.frexp(top)[1] - 1 + 127 - 7, 1), 1, 254)
    codes = (v * np.exp2(127.0 - byte)[:, None, :]).reshape(n, m).astype(np.float32).astype(ml_dtypes.float8_e4m3fn).view(np.uint8)
    words = codes.reshape(n // 512, 128, 4, m).transpose(0, 1, 3, 2)
    return np.ascontiguousarray(words), np.ascontiguousarray(byte.astype(np.uint8).reshape(n // 512, 16, m))


K, T, S, H, C = 512, 2048, 512, 512, 512


def setup_inputs():
    n = np.random.standard_normal
    s = mx_kscale(K)[:, None]
    packed_xT = pack_weight(n((K, T)) * s)
    packed_w1 = pack_weight(n((K, H)) / np.sqrt(K) / s)
    packed_w2 = pack_weight(n((K, H)) / np.sqrt(K) / s)
    return {
        "x_words": packed_xT[0],
        "x_scales": packed_xT[1],
        "w1_words": packed_w1[0],
        "w1_scales": packed_w1[1],
        "w2_words": packed_w2[0],
        "w2_scales": packed_w2[1],
        "gs": (np.random.uniform(0.5, 1.5, (K, 1)) / s).astype(np.float32),
        "offs": striped(np.random.permutation(T)[:S]),
        "two": striped(np.random.permutation(T)[:S]),
        "n1": striped8(np.stack([np.random.permutation(S) for _ in range(8)])),
        "n2": striped8(np.stack([np.random.permutation(S) for _ in range(8)])),
        "n3": striped8(np.stack([np.random.permutation(S) for _ in range(8)])),
        "n4": striped8(np.stack([np.random.permutation(S) for _ in range(8)])),
        "cand": striped(np.random.permutation(T)[:C]),
        "n5": striped8(np.stack([np.random.permutation(S) for _ in range(8)])),
        "n6": striped8(np.stack([np.random.permutation(S) for _ in range(8)])),
    }


def reference(x_words, x_scales, w1_words, w1_scales, w2_words, w2_scales, gs, offs, two, n1, n2, n3, n4, cand, n5, n6):
    x_cand = unpack_weight(x_words, x_scales)[:, unstriped(cand)]
    xq = unpack_weight(x_words, x_scales)[:, unstriped(offs)]
    y = unpack_weight(w1_words, w1_scales).T @ xq
    x_two = unpack_weight(x_words, x_scales)[:, unstriped(two)]
    d = unpack_weight(w2_words, w2_scales).T @ x_two
    z = f64(gs) * (np.maximum(y[np.arange(H)[:, None], runs(n1, H)] + d[np.arange(H)[:, None], runs(n3, H)], y[np.arange(H)[:, None], runs(n2, H)] + d[np.arange(H)[:, None], runs(n4, H)]))
    s = 0.0625 * ((x_cand.T @ mxq(z, 0, "e4m3")))
    pa = s[np.arange(C)[:, None], runs(n5, C)]
    pb = s[np.arange(C)[:, None], runs(n6, C)]
    mu = 0.3125 * (s + pa + pb)
    out_0 = (s - mu) / (np.sqrt((pa - mu) ** 2 + (pb - mu) ** 2 + 0.25))
    return (out_0,) + planes(out_0)

@@ -1,0 +1,244 @@
+from contextlib import ExitStack
+
+import concourse.mybir as mybir
+
+F32 = mybir.dt.float32
+BF16 = mybir.dt.bfloat16
+I32 = mybir.dt.int32
+U32 = mybir.dt.uint32
+U16 = mybir.dt.uint16
+U8 = mybir.dt.uint8
+FP8X4 = mybir.dt.float8_e4m3fn_x4
+ALU = mybir.AluOpType
+ACT = mybir.ActivationFunctionType
+
+P = 128
+T = 2048
+S = 512
+FLOPS = 3 * 2 * 512 * 512 * 512
+Z_CHUNKS = (256, 128, 128)
+O_CHUNKS = (256, 128, 128)
+ROOT_HALF = 0.5 ** 0.5
+
+
+def spans(widths):
+    out = []
+    start = 0
+    for w in widths:
+        out.append((start, w))
+        start = start + w
+    return out
+
+
+def tile_picked_twcpathbstd_none_po_kernel(
+    tc, x_words, x_scales, w1_words, w1_scales, w2_words, w2_scales, gs,
+    offs, two, n1, n2, n3, n4, cand, n5, n6, out_0, out_1, out_2,
+):
+    nc = tc.nc
+    with ExitStack() as ctx:
+        keep = ctx.enter_context(tc.tile_pool(name="keep", bufs=1))
+        psum = ctx.enter_context(tc.psum_pool(name="psum", bufs=1))
+
+        def load_list(src, name):
+            tile = keep.tile([P, S // 16], U16, name=name)
+            nc.sync.dma_start(tile[:], src)
+            return tile
+
+        def load_words(src, width, name):
+            tile = keep.tile([P, width], U32, name=name, align_bytes=64)
+            nc.sync.dma_start(tile[:].bitcast(I32), src[0].rearrange("p n t -> p (n t)").bitcast(I32))
+            return tile
+
+        def load_scales(src, width, name, queue):
+            tile = keep.tile([P, width], U8, name=name, align_bytes=64)
+            nc.vector.memset(tile[:].bitcast(I32), 0)
+            for q in range(4):
+                queue.dma_start(tile[32 * q : 32 * q + 4, :].bitcast(I32), src[0, 4 * q : 4 * q + 4, :].bitcast(I32))
+            return tile
+
+        def deal(src, dtype, run, name):
+            tile = keep.tile([P, S], dtype, name=name, align_bytes=64)
+            nc.vector.tensor_copy(
+                tile[:].rearrange("p (t m i) -> p m t i", t=4, i=run),
+                src[:].rearrange("p (m i t) -> p m t i", t=4, i=run),
+            )
+            return tile
+
+        def pick(lst, name):
+            words = keep.tile([P, S], U32, name=name + "_w", align_bytes=64)
+            scales = keep.tile([P, S], U8, name=name + "_s", align_bytes=64)
+            nc.vector.tensor_copy(words[:], xw[:].indirect(lst[:]))
+            nc.vector.tensor_copy(scales[:], xs[:].indirect(lst[:]))
+            return words, scales
+
+        warm = keep.tile([P, 2], F32, name="warm")
+        nc.vector.memset(warm[:, 0:1], 1.0)
+        nc.scalar.activation(warm[:, 1:2], warm[:, 0:1], ACT.Abs_reciprocal_sqrt)
+
+        w1w = load_words(w1_words, S, "w1w")
+        xw = load_words(x_words, T, "xw")
+        l_offs = load_list(offs, "l_offs")
+        xs = load_scales(x_scales, T, "xs", nc.sync)
+        w1s = load_scales(w1_scales, S, "w1s", nc.sync)
+        l_two = load_list(two, "l_two")
+        w2w = load_words(w2_words, S, "w2w")
+        w2s = load_scales(w2_scales, S, "w2s", nc.sync)
+        l1 = load_list(n1, "l1")
+        l2 = load_list(n2, "l2")
+        l3 = load_list(n3, "l3")
+        l4 = load_list(n4, "l4")
+        gain = keep.tile([P, 4], F32, name="gain")
+        nc.sync.dma_start(gain[:], gs.rearrange("(p t) o -> p (t o)", t=4))
+        l_cand = load_list(cand, "l_cand")
+        l5 = load_list(n5, "l5")
+        l6 = load_list(n6, "l6")
+
+        banks = [psum.tile([P, S], F32, name=f"bank{b}") for b in range(8)]
+
+        w1wd = deal(w1w, U32, 4, "w1wd")
+        xo_w, xo_s = pick(l_offs, "xo")
+        w1sd = deal(w1s, U8, 16, "w1sd")
+        xt_w, xt_s = pick(l_two, "xt")
+        w2wd = deal(w2w, U32, 4, "w2wd")
+        w2sd = deal(w2s, U8, 16, "w2sd")
+
+        def project(ww, ws, xw_, xs_, bank0, name):
+            rows = []
+            for t in range(4):
+                cols = slice(P * t, P * (t + 1))
+                nc.tensor.matmul_mx(
+                    out=banks[bank0 + t][:], lhsT=ww[:, cols].bitcast(FP8X4), lhsT_scale=ws[:, cols],
+                    rhs=xw_[:].bitcast(FP8X4), rhs_scale=xs_[:], start=True, stop=True,
+                )
+                rows.append(keep.tile([P, S], F32, name=f"{name}{t}"))
+            return rows
+
+        y = project(w1wd, w1sd, xo_w, xo_s, 0, "y")
+        d = project(w2wd, w2sd, xt_w, xt_s, 4, "d")
+        nc.scalar.copy(y[0][:], banks[0][:])
+        nc.scalar.copy(y[1][:], banks[1][:])
+        nc.scalar.copy(d[0][:], banks[4][:])
+        nc.scalar.copy(d[1][:], banks[5][:])
+        for t in range(2, 4):
+            nc.scalar.copy(y[t][:], banks[t][:])
+            nc.scalar.copy(d[t][:], banks[4 + t][:])
+
+        xc_w, xc_s = pick(l_cand, "xc")
+        xc_wd = deal(xc_w, U32, 4, "xc_wd")
+        xc_sd = deal(xc_s, U8, 16, "xc_sd")
+
+        zq = keep.tile([P, S], U32, name="zq", align_bytes=64)
+        zs = keep.tile([P, S], U8, name="zs", align_bytes=64)
+        w = [keep.tile([P, S], F32, name=f"w{t}") for t in range(4)]
+
+        def z_gathers(c, j0, n):
+            sl = slice(j0 // 16, (j0 + n) // 16)
+            ya = keep.tile([P, 4, n], F32, name=f"ya{c}")
+            yb = keep.tile([P, 4, n], F32, name=f"yb{c}")
+            sa = keep.tile([P, 4, n], F32, name=f"sa{c}")
+            sb = keep.tile([P, 4, n], F32, name=f"sb{c}")
+            for t in range(4):
+                nc.vector.tensor_copy(ya[:, t, :], y[t][:].indirect(l1[:, sl]))
+                nc.vector.tensor_copy(yb[:, t, :], y[t][:].indirect(l2[:, sl]))
+                nc.vector.tensor_tensor(sa[:, t, :], d[t][:].indirect(l3[:, sl]), ya[:, t, :], ALU.add)
+                nc.vector.tensor_tensor(sb[:, t, :], d[t][:].indirect(l4[:, sl]), yb[:, t, :], ALU.add)
+            big = keep.tile([P, 4, n], F32, name=f"big{c}")
+            nc.vector.tensor_tensor(big[:], sa[:], sb[:], ALU.max)
+            zi = keep.tile([P, n, 4], BF16, name=f"zi{c}", align_bytes=64)
+            if c == len(Z_CHUNKS) - 1:
+                nc.vector.tensor_tensor(
+                    zi[:], big[:].rearrange("p t n -> p n t"), gain[:].unsqueeze(1).to_broadcast([P, n, 4]), ALU.mult
+                )
+            else:
+                zp = keep.tile([P, 4, n], BF16, name=f"zp{c}")
+                for t in range(4):
+                    nc.scalar.activation(zp[:, t, :], big[:, t, :], ACT.Copy, scale=gain[:, t : t + 1])
+                nc.scalar.copy(
+                    zi[:].rearrange("p (c i) t -> p c t i", i=4), zp[:].rearrange("p t (c i) -> p c t i", i=4)
+                )
+            return zi
+
+        def score(zi, j0, n):
+            cs = slice(j0, j0 + n)
+            nc.vector.quantize_mx(out=zq[:, cs].bitcast(FP8X4), scales=zs[:, cs], in_=zi[:].rearrange("p n t -> p (n t)"))
+            for t in range(4):
+                cols = slice(P * t, P * (t + 1))
+                nc.tensor.matmul_mx(
+                    out=banks[t][:, cs], lhsT=xc_wd[:, cols].bitcast(FP8X4), lhsT_scale=xc_sd[:, cols],
+                    rhs=zq[:, cs].bitcast(FP8X4), rhs_scale=zs[:, cs], start=True, stop=True,
+                )
+                nc.scalar.activation(w[t][:, cs], banks[t][:, cs], ACT.Copy, scale=-0.3125 * 0.0625)
+
+        pending = None
+        for c, (j0, n) in enumerate(spans(Z_CHUNKS)):
+            zi = z_gathers(c, j0, n)
+            if pending is not None:
+                score(*pending)
+            pending = (zi, j0, n)
+        score(*pending)
+
+        oq = keep.tile([P, S], U32, name="oq", align_bytes=64)
+        os_ = keep.tile([P, S], U8, name="os_", align_bytes=64)
+        out_rows = out_0.rearrange("(p t) j -> p t j", t=4)
+        out_codes = out_1[0].rearrange("p n t -> p (n t)").bitcast(I32)
+
+        def o_gathers(c, j0, n):
+            sl = slice(j0 // 16, (j0 + n) // 16)
+            ga = keep.tile([P, 4, n], F32, name=f"ga{c}")
+            gd = keep.tile([P, 4, n], F32, name=f"gd{c}")
+            for t in range(4):
+                nc.vector.tensor_copy(ga[:, t, :], w[t][:].indirect(l5[:, sl]))
+            for t in range(4):
+                nc.vector.tensor_tensor(gd[:, t, :], w[t][:].indirect(l6[:, sl]), ga[:, t, :], ALU.subtract)
+            sq_d = keep.tile([P, 4, n], F32, name=f"sq_d{c}")
+            nc.scalar.activation(sq_d[:], gd[:], ACT.Square, scale=3.2 * ROOT_HALF)
+            u = keep.tile([P, 4, n], F32, name=f"u{c}")
+            nc.vector.scalar_tensor_tensor(u[:], ga[:], 2.0, gd[:], ALU.mult, ALU.add)
+            lin = keep.tile([P, 4, n], F32, name=f"lin{c}")
+            num = keep.tile([P, 4, n], F32, name=f"num{c}")
+            for t in range(4):
+                nc.vector.scalar_tensor_tensor(lin[:, t, :], w[t][:, j0 : j0 + n], -5.0 / 3.0, u[:, t, :], ALU.mult, ALU.add)
+            sq_l = keep.tile([P, 4, n], F32, name=f"sq_l{c}")
+            nc.scalar.activation(sq_l[:], lin[:], ACT.Square, scale=1.2 * ROOT_HALF)
+            for t in range(4):
+                nc.vector.scalar_tensor_tensor(num[:, t, :], w[t][:, j0 : j0 + n], -2.2, u[:, t, :], ALU.mult, ALU.add)
+            return c, j0, n, sq_d, sq_l, num
+
+        def o_sum(c, j0, n, sq_d, sq_l, num):
+            q = keep.tile([P, 4, n], F32, name=f"q{c}")
+            nc.vector.scalar_tensor_tensor(q[:], sq_l[:], 0.25, sq_d[:], ALU.add, ALU.add)
+            r = keep.tile([P, 4, n], F32, name=f"r{c}")
+            nc.scalar.activation(r[:], q[:], ACT.Abs_reciprocal_sqrt)
+            return c, j0, n, num, r
+
+        def o_final(c, j0, n, num, r):
+            res = keep.tile([P, 4, n], F32, name=f"res{c}")
+            nc.vector.tensor_tensor(res[:], num[:], r[:], ALU.mult)
+            nc.sync.dma_start(out_rows[:, :, j0 : j0 + n], res[:])
+            ri = keep.tile([P, n, 4], BF16, name=f"ri{c}", align_bytes=64)
+            dst = ri[:].rearrange("p (c i) t -> p c t i", i=4)
+            src = res[:].rearrange("p t (c i) -> p c t i", i=4)
+            if c == len(O_CHUNKS) - 1:
+                nc.vector.tensor_copy(dst, src)
+            else:
+                nc.scalar.copy(dst, src)
+            return ri, j0, n
+
+        def o_planes(ri, j0, n):
+            cs = slice(j0, j0 + n)
+            nc.vector.quantize_mx(out=oq[:, cs].bitcast(FP8X4), scales=os_[:, cs], in_=ri[:].rearrange("p n t -> p (n t)"))
+            nc.sync.dma_start(out_codes[:, cs], oq[:, cs].bitcast(I32))
+
+        stages = [o_sum, o_final, o_planes]
+        state = {}
+        chunks = spans(O_CHUNKS)
+        for step in range(len(chunks) + len(stages)):
+            if step < len(chunks):
+                state[step] = o_gathers(step, *chunks[step])
+            for k, stage in enumerate(stages):
+                c = step - 1 - k
+                if 0 <= c < len(chunks):
+                    state[c] = stage(*state[c])
+        for q in range(4):
+            queue = nc.sync if q % 2 == 0 else nc.scalar
+            queue.dma_start(out_2[0, 4 * q : 4 * q + 4, :].bitcast(I32), os_[32 * q : 32 * q + 4, :].bitcast(I32))

@@ -1,6 +1,7 @@
 from contextlib import ExitStack
 
 import concourse.mybir as mybir
+from concourse.masks import make_identity
 
 F32 = mybir.dt.float32
 BF16 = mybir.dt.bfloat16
@@ -15,19 +16,9 @@ ACT = mybir.ActivationFunctionType
 P = 128
 T = 2048
 S = 512
+BLK = 128
 FLOPS = 3 * 2 * 512 * 512 * 512
-Z_CHUNKS = (256, 128, 128)
-O_CHUNKS = (256, 128, 128)
 ROOT_HALF = 0.5 ** 0.5
-
-
-def spans(widths):
-    out = []
-    start = 0
-    for w in widths:
-        out.append((start, w))
-        start = start + w
-    return out
 
 
 def tile_picked_twcpathbstd_none_po_kernel(
@@ -45,19 +36,17 @@ def tile_picked_twcpathbstd_none_po_kernel(
             return tile
 
         def load_words(src, width, name):
-            tile = keep.tile([P, width], U32, name=name, align_bytes=64)
+            tile = keep.tile([P, width], U32, name=name, tag=name, align_bytes=64)
             nc.sync.dma_start(tile[:].bitcast(I32), src[0].rearrange("p n t -> p (n t)").bitcast(I32))
             return tile
 
-        def load_scales(src, width, name, queue):
-            tile = keep.tile([P, width], U8, name=name, align_bytes=64)
-            nc.vector.memset(tile[:].bitcast(I32), 0)
-            for q in range(4):
-                queue.dma_start(tile[32 * q : 32 * q + 4, :].bitcast(I32), src[0, 4 * q : 4 * q + 4, :].bitcast(I32))
-            return tile
+        def load_scale_rows(tile, src, row0, quadrants):
+            for q in quadrants:
+                rows = tile[32 * q + row0 : 32 * q + row0 + 4, :]
+                nc.sync.dma_start(rows.bitcast(I32), src[0, 4 * q : 4 * q + 4, :].bitcast(I32))
 
         def deal(src, dtype, run, name):
-            tile = keep.tile([P, S], dtype, name=name, align_bytes=64)
+            tile = keep.tile([P, S], dtype, name=name, tag=name, align_bytes=64)
             nc.vector.tensor_copy(
                 tile[:].rearrange("p (t m i) -> p m t i", t=4, i=run),
                 src[:].rearrange("p (m i t) -> p m t i", t=4, i=run),
@@ -71,174 +60,310 @@ def tile_picked_twcpathbstd_none_po_kernel(
             nc.vector.tensor_copy(scales[:], xs[:].indirect(lst[:]))
             return words, scales
 
-        warm = keep.tile([P, 2], F32, name="warm")
-        nc.vector.memset(warm[:, 0:1], 1.0)
-        nc.scalar.activation(warm[:, 1:2], warm[:, 0:1], ACT.Abs_reciprocal_sqrt)
+        xs = keep.tile([P, T], U8, name="xs", align_bytes=64)
+        ws = keep.tile([P, S], U8, name="ws", tag="ws", align_bytes=64)
+        nc.vector.memset(xs[:].bitcast(I32), 0)
+        nc.vector.memset(ws[:].bitcast(I32), 0)
+        quarter = keep.tile([P, 1], F32, name="quarter")
+        warm = keep.tile([P, 1], F32, name="warm")
+        nc.vector.memset(quarter[:], 0.25)
+        floors = [keep.tile([P, 1], F32, name=f"floor{b}", tag=f"floor{b}", align_bytes=64) for b in range(2)]
+        for floor in floors:
+            nc.vector.memset(floor[:], 0.25)
+        nc.scalar.activation(warm[:], quarter[:], ACT.Abs_reciprocal_sqrt, bias=quarter[:])
 
-        w1w = load_words(w1_words, S, "w1w")
-        xw = load_words(x_words, T, "xw")
         l_offs = load_list(offs, "l_offs")
-        xs = load_scales(x_scales, T, "xs", nc.sync)
-        w1s = load_scales(w1_scales, S, "w1s", nc.sync)
+        xw = load_words(x_words, T, "xw")
+        load_scale_rows(xs, x_scales, 0, range(4))
         l_two = load_list(two, "l_two")
+        load_scale_rows(ws, w1_scales, 0, range(2))
+        w1w = load_words(w1_words, S, "w1w")
         w2w = load_words(w2_words, S, "w2w")
-        w2s = load_scales(w2_scales, S, "w2s", nc.sync)
+        load_scale_rows(ws, w1_scales, 0, range(2, 4))
+        load_scale_rows(ws, w2_scales, 4, range(4))
+        l_cand = load_list(cand, "l_cand")
         l1 = load_list(n1, "l1")
         l2 = load_list(n2, "l2")
         l3 = load_list(n3, "l3")
         l4 = load_list(n4, "l4")
         gain = keep.tile([P, 4], F32, name="gain")
         nc.sync.dma_start(gain[:], gs.rearrange("(p t) o -> p (t o)", t=4))
-        l_cand = load_list(cand, "l_cand")
         l5 = load_list(n5, "l5")
         l6 = load_list(n6, "l6")
 
         banks = [psum.tile([P, S], F32, name=f"bank{b}") for b in range(8)]
+        ident = keep.tile([P, P], F32, name="ident")
+        make_identity(nc, ident[:])
 
-        w1wd = deal(w1w, U32, 4, "w1wd")
         xo_w, xo_s = pick(l_offs, "xo")
-        w1sd = deal(w1s, U8, 16, "w1sd")
+        w1wd = deal(w1w, U32, 4, "w1wd")
+        wsd = deal(ws, U8, 16, "wsd")
         xt_w, xt_s = pick(l_two, "xt")
         w2wd = deal(w2w, U32, 4, "w2wd")
-        w2sd = deal(w2s, U8, 16, "w2sd")
 
-        def project(ww, ws, xw_, xs_, bank0, name):
+        def project(ww, row0, xw_, xs_, bank0, name):
             rows = []
             for t in range(4):
                 cols = slice(P * t, P * (t + 1))
                 nc.tensor.matmul_mx(
-                    out=banks[bank0 + t][:], lhsT=ww[:, cols].bitcast(FP8X4), lhsT_scale=ws[:, cols],
+                    out=banks[bank0 + t][:], lhsT=ww[:, cols].bitcast(FP8X4), lhsT_scale=wsd[row0:P, cols],
                     rhs=xw_[:].bitcast(FP8X4), rhs_scale=xs_[:], start=True, stop=True,
                 )
-                rows.append(keep.tile([P, S], F32, name=f"{name}{t}"))
+                row = keep.tile([P, 2 * S if t < 2 else S], F32, name=f"{name}{t}")
+                if t < 2:
+                    nc.vector.memset(row[:, S:], 0.0)
+                rows.append(row)
             return rows
 
-        y = project(w1wd, w1sd, xo_w, xo_s, 0, "y")
-        d = project(w2wd, w2sd, xt_w, xt_s, 4, "d")
-        nc.scalar.copy(y[0][:], banks[0][:])
-        nc.scalar.copy(y[1][:], banks[1][:])
-        nc.scalar.copy(d[0][:], banks[4][:])
-        nc.scalar.copy(d[1][:], banks[5][:])
-        for t in range(2, 4):
-            nc.scalar.copy(y[t][:], banks[t][:])
-            nc.scalar.copy(d[t][:], banks[4 + t][:])
+        y = project(w1wd, 0, xo_w, xo_s, 0, "y")
+        d = project(w2wd, 4, xt_w, xt_s, 4, "d")
+        for pair in ((0, 1), (2, 3)):
+            for t in pair:
+                nc.scalar.copy(y[t][:, :S], banks[t][:])
+            for t in pair:
+                nc.scalar.copy(d[t][:, :S], banks[4 + t][:])
 
-        xc_w, xc_s = pick(l_cand, "xc")
-        xc_wd = deal(xc_w, U32, 4, "xc_wd")
+        xc_wd = keep.tile([P, S], U32, name="xc_wd", tag="w2w", align_bytes=64)
+        xc_s = keep.tile([P, S], U8, name="xc_s", tag="ws", align_bytes=64)
+        nc.vector.tensor_copy(xc_wd[:].rearrange("p (t m) -> p m t", t=4), xw[:].indirect(l_cand[:]))
+        nc.vector.tensor_copy(xc_s[:], xs[:].indirect(l_cand[:]))
         xc_sd = deal(xc_s, U8, 16, "xc_sd")
 
+        def turn(bank, part, ts, start, stop):
+            for k, t in enumerate(ts):
+                nc.tensor.matmul(
+                    bank[:, P * k : P * (k + 1)], lhsT=part[:, t, :], rhs=ident[:], is_transpose=True,
+                    start=(start and k == 0), stop=(stop and k == len(ts) - 1),
+                )
+
+        def quad(name, dtype=F32, n=BLK, tag=None, rows=4):
+            return keep.tile([P, rows, n], dtype, name=name, tag=tag or name, align_bytes=64)
+
+        def flat(tile):
+            return tile[:].rearrange("p t n -> p (t n)")
+
+        def weave(engine_copy, src, name, n=BLK, tag=None):
+            dst = keep.tile([P, n, 4], BF16, name=name, tag=tag or name, align_bytes=64)
+            engine_copy(dst[:].rearrange("p (c i) t -> p c t i", i=4), src.rearrange("p t (c i) -> p c t i", i=4))
+            return dst
+
         zq = keep.tile([P, S], U32, name="zq", align_bytes=64)
-        zs = keep.tile([P, S], U8, name="zs", align_bytes=64)
+        zs = keep.tile([P, S], U8, name="zs", tag="zs", align_bytes=64)
         w = [keep.tile([P, S], F32, name=f"w{t}") for t in range(4)]
+        s3 = {}
+        last = S // BLK - 1
 
-        def z_gathers(c, j0, n):
-            sl = slice(j0 // 16, (j0 + n) // 16)
-            ya = keep.tile([P, 4, n], F32, name=f"ya{c}")
-            yb = keep.tile([P, 4, n], F32, name=f"yb{c}")
-            sa = keep.tile([P, 4, n], F32, name=f"sa{c}")
-            sb = keep.tile([P, 4, n], F32, name=f"sb{c}")
-            for t in range(4):
-                nc.vector.tensor_copy(ya[:, t, :], y[t][:].indirect(l1[:, sl]))
-                nc.vector.tensor_copy(yb[:, t, :], y[t][:].indirect(l2[:, sl]))
-                nc.vector.tensor_tensor(sa[:, t, :], d[t][:].indirect(l3[:, sl]), ya[:, t, :], ALU.add)
-                nc.vector.tensor_tensor(sb[:, t, :], d[t][:].indirect(l4[:, sl]), yb[:, t, :], ALU.add)
-            big = keep.tile([P, 4, n], F32, name=f"big{c}")
-            nc.vector.tensor_tensor(big[:], sa[:], sb[:], ALU.max)
-            zi = keep.tile([P, n, 4], BF16, name=f"zi{c}", align_bytes=64)
-            if c == len(Z_CHUNKS) - 1:
-                nc.vector.tensor_tensor(
-                    zi[:], big[:].rearrange("p t n -> p n t"), gain[:].unsqueeze(1).to_broadcast([P, n, 4]), ALU.mult
-                )
-            else:
-                zp = keep.tile([P, 4, n], BF16, name=f"zp{c}")
+        zp_a, zp_b = quad("zp_a", BF16, n=256), quad("zp_b", BF16)
+        end = quad("end")
+
+        def z_wide():
+            ya, first, yb, gap = (quad(name, n=S, rows=2) for name in ("ya", "first", "yb", "gap"))
+            for t in range(2):
+                nc.vector.tensor_copy(ya[:, t, :], y[t][:].indirect(l1[:]))
+            for t in range(2):
+                nc.vector.tensor_tensor(first[:, t, :], d[t][:].indirect(l3[:]), ya[:, t, :], ALU.add)
+            for t in range(2):
+                nc.vector.tensor_tensor(yb[:, t, :], y[t][:].indirect(l2[:]), first[:, t, :], ALU.subtract)
+            for t in range(2):
+                nc.vector.tensor_tensor(gap[:, t, :], d[t][:].indirect(l4[:]), yb[:, t, :], ALU.add)
+            for t in range(2):
+                rise, turned = quad(f"rise{t}"), quad(f"turned{t}")
+                across, back = banks[t], banks[2 + t]
+                turn(across, first[:, t, :].rearrange("p (b j) -> p b j", b=4), range(4), True, False)
+                nc.scalar.activation(flat(rise), gap[:, t, :], ACT.Relu)
+                turn(across, rise, range(4), False, True)
+                nc.scalar.copy(flat(turned), across[:])
+                turn(back, turned, range(4), True, True)
+                nc.scalar.activation(zp_a[:, t, :], back[:, :256], ACT.Copy, scale=gain[:, t : t + 1])
+                nc.scalar.activation(zp_b[:, t, :], back[:, 256:384], ACT.Copy, scale=gain[:, t : t + 1])
+                nc.scalar.copy(end[:, t, :], back[:, S - BLK :])
+
+        def fetch_y(out, k, j0):
+            n = out.shape[1]
+            nc.vector.tensor_copy(out, y[2 + k % 2][:].indirect((l1, l2)[k // 2][:, j0 // 16 : (j0 + n) // 16]))
+
+        def add_d(out, other, k, j0):
+            n = out.shape[1]
+            window = d[2 + k % 2][:].indirect((l3, l4)[k // 2][:, j0 // 16 : (j0 + n) // 16])
+            nc.vector.tensor_tensor(out, window, other, ALU.add)
+
+        def scale_plane(planes, t, big):
+            nc.scalar.activation(planes[:, t, :], big, ACT.Copy, scale=gain[:, t : t + 1])
+
+        def row(name, n, tag=None):
+            return keep.tile([P, n], F32, name=name, tag=tag or name, align_bytes=64)
+
+        def score_bank(b, t):
+            return banks[(3, 2, 1, 7)[t]] if b == last else banks[4 + b]
+
+        def z_score(zi, j0, n):
+            nc.vector.quantize_mx(
+                out=zq[:, j0 : j0 + n].bitcast(FP8X4), scales=zs[:, j0 : j0 + n], in_=zi[:].rearrange("p n t -> p (n t)")
+            )
+            for b in range(j0 // BLK, (j0 + n) // BLK):
+                cs = slice(b * BLK, (b + 1) * BLK)
                 for t in range(4):
-                    nc.scalar.activation(zp[:, t, :], big[:, t, :], ACT.Copy, scale=gain[:, t : t + 1])
-                nc.scalar.copy(
-                    zi[:].rearrange("p (c i) t -> p c t i", i=4), zp[:].rearrange("p t (c i) -> p c t i", i=4)
-                )
-            return zi
+                    cols = slice(P * t, P * (t + 1))
+                    nc.tensor.matmul_mx(
+                        out=score_bank(b, t)[:, cols], lhsT=xc_wd[:, cols].bitcast(FP8X4), lhsT_scale=xc_sd[:, cols],
+                        rhs=zq[:, cs].bitcast(FP8X4), rhs_scale=zs[:, cs], start=True, stop=True,
+                    )
+                for t in range(4):
+                    nc.scalar.activation(
+                        w[t][:, cs], score_bank(b, t)[:, P * t : P * (t + 1)], ACT.Copy, scale=-0.3125 * 0.0625
+                    )
 
-        def score(zi, j0, n):
-            cs = slice(j0, j0 + n)
-            nc.vector.quantize_mx(out=zq[:, cs].bitcast(FP8X4), scales=zs[:, cs], in_=zi[:].rearrange("p n t -> p (n t)"))
-            for t in range(4):
-                cols = slice(P * t, P * (t + 1))
-                nc.tensor.matmul_mx(
-                    out=banks[t][:, cs], lhsT=xc_wd[:, cols].bitcast(FP8X4), lhsT_scale=xc_sd[:, cols],
-                    rhs=zq[:, cs].bitcast(FP8X4), rhs_scale=zs[:, cs], start=True, stop=True,
+        def own_term(b, tile):
+            s3[b] = tile
+            for lo, hi in ((0, 1), (1, 2), (2, 3), (3, 4)) if b == last else ((0, 4),):
+                nc.scalar.activation(
+                    flat(s3[b])[:, P * lo : P * hi], score_bank(b, lo)[:, P * lo : P * hi], ACT.Copy,
+                    scale=0.3125 * 0.0625 * 5.0 / 3.0,
                 )
-                nc.scalar.activation(w[t][:, cs], banks[t][:, cs], ACT.Copy, scale=-0.3125 * 0.0625)
 
-        pending = None
-        for c, (j0, n) in enumerate(spans(Z_CHUNKS)):
-            zi = z_gathers(c, j0, n)
-            if pending is not None:
-                score(*pending)
-            pending = (zi, j0, n)
-        score(*pending)
+        z_wide()
+        ys = [row(f"yA{k}", 256, tag) for k, tag in enumerate(("ya", "yb", "first", "gap"))]
+        late = row("late", 256 + 4 * BLK, "turned1")
+        sums = [row("dA0", 256)[:], row("dA1", 256, "turned0")[:], row("dA2", 256)[:], late[:, :256]]
+        for t in range(2):
+            for k in (t, 2 + t):
+                fetch_y(ys[k][:], k, 0)
+            for k in (t, 2 + t):
+                add_d(sums[k], ys[k][:], k, 0)
+            big = row(f"bigA{t}", 256, "rise1" if t == 0 else None)
+            nc.vector.tensor_tensor(big[:], sums[t], sums[2 + t], ALU.max)
+            scale_plane(zp_a, 2 + t, big[:])
+        zi_a = weave(nc.scalar.copy, zp_a[:], "ziA", 256)
+
+        sums, big = quad("dB"), quad("bigB", rows=2)
+        for k in range(4):
+            fetch_y(late[:, 256 + BLK * k : 256 + BLK * (k + 1)], k, 256)
+        for k in range(4):
+            add_d(sums[:, k, :], late[:, 256 + BLK * k : 256 + BLK * (k + 1)], k, 256)
+        nc.vector.tensor_tensor(big[:], sums[:, 0:2, :], sums[:, 2:4, :], ALU.max)
+        for t in range(2):
+            scale_plane(zp_b, 2 + t, big[:, t, :])
+        zi_b = weave(nc.scalar.copy, zp_b[:], "ziB")
+        z_score(zi_a, 0, 256)
+
+        ys, sums = quad("yC", tag="zp_a"), [quad("dC0", rows=2)]
+        for k in range(4):
+            fetch_y(ys[:, k, :], k, 384)
+        for k in range(2):
+            add_d(sums[0][:, k, :], ys[:, k, :], k, 384)
+        z_score(zi_b, 256, BLK)
+        sums.append(quad("dC1", rows=2, tag="zp_b"))
+        for k in range(2, 4):
+            add_d(sums[1][:, k - 2, :], ys[:, k, :], k, 384)
+        nc.vector.tensor_tensor(end[:, 2:4, :], sums[0][:], sums[1][:], ALU.max)
+        zi_c = keep.tile([P, BLK, 4], BF16, name="ziC", align_bytes=64)
+        nc.vector.tensor_tensor(
+            zi_c[:].rearrange("p (c i) t -> p c t i", i=4), end[:].rearrange("p t (c i) -> p c t i", i=4),
+            gain[:].unsqueeze(1).unsqueeze(3).to_broadcast([P, BLK // 4, 4, 4]), ALU.mult,
+        )
+        z_score(zi_c, 384, BLK)
+        for b, tag in ((0, None), (3, "zs"), (1, "xc_sd"), (2, "w2w")):
+            own_term(b, quad(f"s3_{b}", tag=tag))
 
         oq = keep.tile([P, S], U32, name="oq", align_bytes=64)
         os_ = keep.tile([P, S], U8, name="os_", align_bytes=64)
         out_rows = out_0.rearrange("(p t) j -> p t j", t=4)
         out_codes = out_1[0].rearrange("p n t -> p (n t)").bitcast(I32)
+        res = [quad(f"res{b}") for b in range(4)]
 
-        def o_gathers(c, j0, n):
+        def o_gathers(name, ts, j0, n, ga_after, neg_after, sum_after):
             sl = slice(j0 // 16, (j0 + n) // 16)
-            ga = keep.tile([P, 4, n], F32, name=f"ga{c}")
-            gd = keep.tile([P, 4, n], F32, name=f"gd{c}")
-            for t in range(4):
-                nc.vector.tensor_copy(ga[:, t, :], w[t][:].indirect(l5[:, sl]))
-            for t in range(4):
-                nc.vector.tensor_tensor(gd[:, t, :], w[t][:].indirect(l6[:, sl]), ga[:, t, :], ALU.subtract)
-            sq_d = keep.tile([P, 4, n], F32, name=f"sq_d{c}")
-            nc.scalar.activation(sq_d[:], gd[:], ACT.Square, scale=3.2 * ROOT_HALF)
-            u = keep.tile([P, 4, n], F32, name=f"u{c}")
-            nc.vector.scalar_tensor_tensor(u[:], ga[:], 2.0, gd[:], ALU.mult, ALU.add)
-            lin = keep.tile([P, 4, n], F32, name=f"lin{c}")
-            num = keep.tile([P, 4, n], F32, name=f"num{c}")
-            for t in range(4):
-                nc.vector.scalar_tensor_tensor(lin[:, t, :], w[t][:, j0 : j0 + n], -5.0 / 3.0, u[:, t, :], ALU.mult, ALU.add)
-            sq_l = keep.tile([P, 4, n], F32, name=f"sq_l{c}")
+            m = len(ts)
+            ga, u = quad(f"ga{name}", n=n, rows=m, tag=ga_after), quad(f"u{name}", n=n, rows=m, tag=sum_after)
+            for k, t in enumerate(ts):
+                nc.vector.tensor_copy(ga[:, k, :], w[t][:].indirect(l5[:, sl]))
+            neg = ga
+            if name != "3":
+                neg = quad(f"neg{name}", n=n, rows=m, tag=neg_after)
+                nc.scalar.activation(neg[:], ga[:], ACT.Copy, scale=-2.0)
+            for k, t in enumerate(ts):
+                nc.vector.tensor_tensor(u[:, k, :], w[t][:].indirect(l6[:, sl]), ga[:, k, :], ALU.add)
+            return neg, u
+
+        def o_front(name, b, ts, neg, u, lin, diff, num_after=None):
+            m = len(ts)
+            own = range(m)
+            num, sq_d, sq_l = quad(f"num{name}", rows=m, tag=num_after), quad(f"sq_d{name}", rows=m), quad(f"sq_l{name}", rows=m)
+            turn(lin, s3[b], ts, True, False)
+            turn(diff, neg, own, True, False)
+            turn(lin, u, own, False, True)
+            nc.scalar.activation(flat(sq_l), lin[:, : m * P], ACT.Square, scale=1.2 * ROOT_HALF)
+            turn(diff, u, own, False, True)
+            nc.scalar.activation(flat(sq_d), diff[:, : m * P], ACT.Square, scale=3.2 * ROOT_HALF)
+            nc.vector.scalar_tensor_tensor(num[:], s3[b][:, ts[0] : ts[0] + m, :], 1.32, u, ALU.mult, ALU.add)
+            return name, b, ts, sq_d, sq_l, num
+
+        def o_sum(name, b, ts, sq_d, sq_l, num, bank):
+            m = len(ts)
+            r = quad(f"r{name}", rows=m)
+            turn(bank, sq_l, range(m), True, False)
+            turn(bank, sq_d, range(m), False, True)
+            nc.scalar.activation(flat(r), bank[:, : m * P], ACT.Abs_reciprocal_sqrt, bias=(floors + [quarter])[b][:])
+            return b, ts, num, r
+
+        def o_front_direct(name, ts, ga, u, after):
+            own = s3[last][:, ts[0] : ts[0] + 2, :]
+            lin, diff = after[:, 0:2, :], after[:, 2:4, :]
+            num, sq_d, sq_l = quad(f"num{name}", rows=2), quad(f"sq_d{name}", rows=2), quad(f"sq_l{name}", rows=2)
+            nc.vector.tensor_tensor(lin[:], u, own, ALU.add)
             nc.scalar.activation(sq_l[:], lin[:], ACT.Square, scale=1.2 * ROOT_HALF)
-            for t in range(4):
-                nc.vector.scalar_tensor_tensor(num[:, t, :], w[t][:, j0 : j0 + n], -2.2, u[:, t, :], ALU.mult, ALU.add)
-            return c, j0, n, sq_d, sq_l, num
+            nc.vector.scalar_tensor_tensor(diff[:], ga, -2.0, u, ALU.mult, ALU.add)
+            nc.scalar.activation(sq_d[:], diff[:], ACT.Square, scale=3.2 * ROOT_HALF)
+            nc.vector.scalar_tensor_tensor(num[:], own, 1.32, u, ALU.mult, ALU.add)
+            return name, ts, sq_d, sq_l, num
 
-        def o_sum(c, j0, n, sq_d, sq_l, num):
-            q = keep.tile([P, 4, n], F32, name=f"q{c}")
-            nc.vector.scalar_tensor_tensor(q[:], sq_l[:], 0.25, sq_d[:], ALU.add, ALU.add)
-            r = keep.tile([P, 4, n], F32, name=f"r{c}")
-            nc.scalar.activation(r[:], q[:], ACT.Abs_reciprocal_sqrt)
-            return c, j0, n, num, r
+        def o_sum_direct(name, ts, sq_d, sq_l, num):
+            q, r = quad(f"q{name}", rows=2), quad(f"r{name}", rows=2)
+            nc.vector.tensor_tensor(q[:], sq_l[:], sq_d[:], ALU.add)
+            nc.scalar.activation(r[:], q[:], ACT.Abs_reciprocal_sqrt, bias=quarter[:])
+            return last, ts, num, r
 
-        def o_final(c, j0, n, num, r):
-            res = keep.tile([P, 4, n], F32, name=f"res{c}")
-            nc.vector.tensor_tensor(res[:], num[:], r[:], ALU.mult)
-            nc.sync.dma_start(out_rows[:, :, j0 : j0 + n], res[:])
-            ri = keep.tile([P, n, 4], BF16, name=f"ri{c}", align_bytes=64)
-            dst = ri[:].rearrange("p (c i) t -> p c t i", i=4)
-            src = res[:].rearrange("p t (c i) -> p c t i", i=4)
-            if c == len(O_CHUNKS) - 1:
-                nc.vector.tensor_copy(dst, src)
-            else:
-                nc.scalar.copy(dst, src)
-            return ri, j0, n
+        def o_final(b, ts, num, r):
+            rows = slice(ts[0], ts[0] + len(ts))
+            nc.vector.tensor_tensor(res[b][:, rows, :], num[:], r[:], ALU.mult)
+            nc.sync.dma_start(out_rows[:, rows, b * BLK : (b + 1) * BLK], res[b][:, rows, :])
 
-        def o_planes(ri, j0, n):
-            cs = slice(j0, j0 + n)
+        def o_weave(b, after=None):
+            return weave(nc.vector.tensor_copy if b >= last - 1 else nc.scalar.copy, res[b][:], f"ri{b}", tag=after)
+
+        def o_planes(b, ri):
+            cs = slice(b * BLK, (b + 1) * BLK)
             nc.vector.quantize_mx(out=oq[:, cs].bitcast(FP8X4), scales=os_[:, cs], in_=ri[:].rearrange("p n t -> p (n t)"))
             nc.sync.dma_start(out_codes[:, cs], oq[:, cs].bitcast(I32))
 
-        stages = [o_sum, o_final, o_planes]
-        state = {}
-        chunks = spans(O_CHUNKS)
-        for step in range(len(chunks) + len(stages)):
-            if step < len(chunks):
-                state[step] = o_gathers(step, *chunks[step])
-            for k, stage in enumerate(stages):
-                c = step - 1 - k
-                if 0 <= c < len(chunks):
-                    state[c] = stage(*state[c])
+        whole = [0, 1, 2, 3]
+        neg, u = o_gathers("0", whole, 0, BLK, None, None, None)
+        f0 = o_front("0", 0, whole, neg[:], u[:], banks[0], banks[1])
+        s0 = o_sum(*f0, banks[2])
+        neg, u = o_gathers("1", whole, BLK, BLK, "ga0", "u0", None)
+        f1 = o_front("1", 1, whole, neg[:], u[:], banks[1], banks[0])
+        o_final(*s0)
+        s1 = o_sum(*f1, banks[4])
+        r0 = o_weave(0, "sq_l1")
+        neg, u = o_gathers("2", whole, 256, BLK, "floor0", "u1", None)
+        f2 = o_front("2", 2, whole, neg[:], u[:], banks[0], banks[1])
+        o_planes(0, r0)
+        o_final(*s1)
+        s2 = o_sum(*f2, banks[2])
+        r1 = o_weave(1, "sq_l2")
+        ga, u = o_gathers("3", whole, 384, BLK, "floor1", None, None)
+        forms = quad("forms", rows=8, tag="sq_d2")
+        f3a = o_front_direct("3a", [0, 1], ga[:, 0:2, :], u[:, 0:2, :], forms[:, 0:4, :])
+        f3b = o_front_direct("3b", [2, 3], ga[:, 2:4, :], u[:, 2:4, :], forms[:, 4:8, :])
+        o_planes(1, r1)
+        o_final(*s2)
+        s3a = o_sum_direct(*f3a)
+        s3b = o_sum_direct(*f3b)
+        r2 = o_weave(2)
+        o_final(*s3a)
+        o_final(*s3b)
+        o_planes(2, r2)
+        o_planes(3, o_weave(3))
         for q in range(4):
             queue = nc.sync if q % 2 == 0 else nc.scalar
             queue.dma_start(out_2[0, 4 * q : 4 * q + 4, :].bitcast(I32), os_[32 * q : 32 * q + 4, :].bitcast(I32))

@@ -62,7 +62,6 @@ def tile_picked_twcpathbstd_none_po_kernel(
 
         xs = keep.tile([P, T], U8, name="xs", align_bytes=64)
         ws = keep.tile([P, S], U8, name="ws", tag="ws", align_bytes=64)
-        nc.vector.memset(xs[:].bitcast(I32), 0)
         nc.vector.memset(ws[:].bitcast(I32), 0)
         quarter = keep.tile([P, 1], F32, name="quarter")
         warm = keep.tile([P, 1], F32, name="warm")
@@ -72,19 +71,20 @@ def tile_picked_twcpathbstd_none_po_kernel(
             nc.vector.memset(floor[:], 0.25)
         nc.scalar.activation(warm[:], quarter[:], ACT.Abs_reciprocal_sqrt, bias=quarter[:])
 
+        for q in range(4):
+            rows = x_scales[0, 4 * q : 4 * q + 4, :].bitcast(I32)
+            nc.sync.dma_start(xs[32 * q : 32 * q + 32, :].bitcast(I32), rows.partition_broadcast(8))
         l_offs = load_list(offs, "l_offs")
-        xw = load_words(x_words, T, "xw")
-        load_scale_rows(xs, x_scales, 0, range(4))
         l_two = load_list(two, "l_two")
-        load_scale_rows(ws, w1_scales, 0, range(2))
+        l_cand = load_list(cand, "l_cand")
+        xw = load_words(x_words, T, "xw")
         w1w = load_words(w1_words, S, "w1w")
         w2w = load_words(w2_words, S, "w2w")
-        load_scale_rows(ws, w1_scales, 0, range(2, 4))
+        load_scale_rows(ws, w1_scales, 0, range(4))
         load_scale_rows(ws, w2_scales, 4, range(4))
-        l_cand = load_list(cand, "l_cand")
         l1 = load_list(n1, "l1")
-        l2 = load_list(n2, "l2")
         l3 = load_list(n3, "l3")
+        l2 = load_list(n2, "l2")
         l4 = load_list(n4, "l4")
         gain = keep.tile([P, 4], F32, name="gain")
         nc.sync.dma_start(gain[:], gs.rearrange("(p t) o -> p (t o)", t=4))
@@ -98,8 +98,12 @@ def tile_picked_twcpathbstd_none_po_kernel(
         xo_w, xo_s = pick(l_offs, "xo")
         w1wd = deal(w1w, U32, 4, "w1wd")
         wsd = deal(ws, U8, 16, "wsd")
-        xt_w, xt_s = pick(l_two, "xt")
         w2wd = deal(w2w, U32, 4, "w2wd")
+        later = keep.tile([P, 2 * S], U32, name="later", tag="ws", align_bytes=64)
+        xt_w, xc_wd = later[:, :S], later[:, S:]
+        xt_s = keep.tile([P, S], U8, name="xt_s", align_bytes=64)
+        nc.vector.tensor_copy(xt_w, xw[:].indirect(l_two[:]))
+        nc.vector.tensor_copy(xt_s[:], xs[:].indirect(l_two[:]))
 
         def project(ww, row0, xw_, xs_, bank0, name):
             rows = []
@@ -111,7 +115,7 @@ def tile_picked_twcpathbstd_none_po_kernel(
                 )
                 row = keep.tile([P, 2 * S if t < 2 else S], F32, name=f"{name}{t}")
                 if t < 2:
-                    nc.vector.memset(row[:, S:], 0.0)
+                    (nc.vector if name == "y" else nc.gpsimd).memset(row[:, S:], 0.0)
                 rows.append(row)
             return rows
 
@@ -123,8 +127,7 @@ def tile_picked_twcpathbstd_none_po_kernel(
             for t in pair:
                 nc.scalar.copy(d[t][:, :S], banks[4 + t][:])
 
-        xc_wd = keep.tile([P, S], U32, name="xc_wd", tag="w2w", align_bytes=64)
-        xc_s = keep.tile([P, S], U8, name="xc_s", tag="ws", align_bytes=64)
+        xc_s = keep.tile([P, S], U8, name="xc_s", align_bytes=64)
         nc.vector.tensor_copy(xc_wd[:].rearrange("p (t m) -> p m t", t=4), xw[:].indirect(l_cand[:]))
         nc.vector.tensor_copy(xc_s[:], xs[:].indirect(l_cand[:]))
         xc_sd = deal(xc_s, U8, 16, "xc_sd")
@@ -262,7 +265,7 @@ def tile_picked_twcpathbstd_none_po_kernel(
             gain[:].unsqueeze(1).unsqueeze(3).to_broadcast([P, BLK // 4, 4, 4]), ALU.mult,
         )
         z_score(zi_c, 384, BLK)
-        for b, tag in ((0, None), (3, "zs"), (1, "xc_sd"), (2, "w2w")):
+        for b, tag in ((0, None), (3, "zs"), (1, "xc_sd"), (2, "ws")):
             own_term(b, quad(f"s3_{b}", tag=tag))
 
         oq = keep.tile([P, S], U32, name="oq", align_bytes=64)
@@ -271,19 +274,23 @@ def tile_picked_twcpathbstd_none_po_kernel(
         out_codes = out_1[0].rearrange("p n t -> p (n t)").bitcast(I32)
         res = [quad(f"res{b}") for b in range(4)]
 
-        def o_gathers(name, ts, j0, n, ga_after, neg_after, sum_after):
-            sl = slice(j0 // 16, (j0 + n) // 16)
-            m = len(ts)
-            ga, u = quad(f"ga{name}", n=n, rows=m, tag=ga_after), quad(f"u{name}", n=n, rows=m, tag=sum_after)
-            for k, t in enumerate(ts):
-                nc.vector.tensor_copy(ga[:, k, :], w[t][:].indirect(l5[:, sl]))
-            neg = ga
-            if name != "3":
-                neg = quad(f"neg{name}", n=n, rows=m, tag=neg_after)
-                nc.scalar.activation(neg[:], ga[:], ACT.Copy, scale=-2.0)
-            for k, t in enumerate(ts):
-                nc.vector.tensor_tensor(u[:, k, :], w[t][:].indirect(l6[:, sl]), ga[:, k, :], ALU.add)
-            return neg, u
+        def first_places(name, j0, after):
+            ga = quad(name, n=2 * BLK, tag=after)
+            for t in range(4):
+                nc.vector.tensor_copy(ga[:, t, :], w[t][:].indirect(l5[:, j0 // 16 : (j0 + 2 * BLK) // 16]))
+            return ga[:, :, :BLK], ga[:, :, BLK:]
+
+        def doubled(name, ga, after):
+            neg = quad(name, tag=after, rows=ga.shape[1])
+            nc.scalar.activation(neg[:], ga, ACT.Copy, scale=-2.0)
+            return neg[:]
+
+        def both_places(b, ga, after):
+            u = quad(f"u{b}", tag=after)
+            for t in range(4):
+                window = w[t][:].indirect(l6[:, b * BLK // 16 : (b + 1) * BLK // 16])
+                nc.vector.tensor_tensor(u[:, t, :], window, ga[:, t, :], ALU.add)
+            return u[:]
 
         def o_front(name, b, ts, neg, u, lin, diff, num_after=None):
             m = len(ts)
@@ -337,24 +344,24 @@ def tile_picked_twcpathbstd_none_po_kernel(
             nc.sync.dma_start(out_codes[:, cs], oq[:, cs].bitcast(I32))
 
         whole = [0, 1, 2, 3]
-        neg, u = o_gathers("0", whole, 0, BLK, None, None, None)
-        f0 = o_front("0", 0, whole, neg[:], u[:], banks[0], banks[1])
+        ga0, ga1 = first_places("ga01", 0, None)
+        neg0, neg1 = doubled("neg0", ga0, None), doubled("neg1", ga1, None)
+        f0 = o_front("0", 0, whole, neg0, both_places(0, ga0, None), banks[0], banks[1])
         s0 = o_sum(*f0, banks[2])
-        neg, u = o_gathers("1", whole, BLK, BLK, "ga0", "u0", None)
-        f1 = o_front("1", 1, whole, neg[:], u[:], banks[1], banks[0])
+        f1 = o_front("1", 1, whole, neg1, both_places(1, ga1, None), banks[1], banks[0])
+        ga2, ga3 = first_places("ga23", 256, "neg0")
         o_final(*s0)
         s1 = o_sum(*f1, banks[4])
         r0 = o_weave(0, "sq_l1")
-        neg, u = o_gathers("2", whole, 256, BLK, "floor0", "u1", None)
-        f2 = o_front("2", 2, whole, neg[:], u[:], banks[0], banks[1])
+        f2 = o_front("2", 2, whole, doubled("neg2", ga2, "u1"), both_places(2, ga2, "floor0"), banks[0], banks[1])
         o_planes(0, r0)
         o_final(*s1)
         s2 = o_sum(*f2, banks[2])
         r1 = o_weave(1, "sq_l2")
-        ga, u = o_gathers("3", whole, 384, BLK, "floor1", None, None)
+        u = both_places(3, ga3, "floor1")
         forms = quad("forms", rows=8, tag="sq_d2")
-        f3a = o_front_direct("3a", [0, 1], ga[:, 0:2, :], u[:, 0:2, :], forms[:, 0:4, :])
-        f3b = o_front_direct("3b", [2, 3], ga[:, 2:4, :], u[:, 2:4, :], forms[:, 4:8, :])
+        f3a = o_front_direct("3a", [0, 1], ga3[:, 0:2, :], u[:, 0:2, :], forms[:, 0:4, :])
+        f3b = o_front_direct("3b", [2, 3], ga3[:, 2:4, :], u[:, 2:4, :], forms[:, 4:8, :])
         o_planes(1, r1)
         o_final(*s2)
         s3a = o_sum_direct(*f3a)

from contextlib import ExitStack

import concourse.mybir as mybir
from concourse.masks import make_identity

F32 = mybir.dt.float32
BF16 = mybir.dt.bfloat16
I32 = mybir.dt.int32
U32 = mybir.dt.uint32
U16 = mybir.dt.uint16
U8 = mybir.dt.uint8
FP8X4 = mybir.dt.float8_e4m3fn_x4
ALU = mybir.AluOpType
ACT = mybir.ActivationFunctionType

P = 128
T = 2048
S = 512
BLK = 128
FLOPS = 3 * 2 * 512 * 512 * 512
ROOT_HALF = 0.5 ** 0.5


def tile_picked_twcpathbstd_none_po_kernel(
    tc, x_words, x_scales, w1_words, w1_scales, w2_words, w2_scales, gs,
    offs, two, n1, n2, n3, n4, cand, n5, n6, out_0, out_1, out_2,
):
    nc = tc.nc
    with ExitStack() as ctx:
        keep = ctx.enter_context(tc.tile_pool(name="keep", bufs=1))
        psum = ctx.enter_context(tc.psum_pool(name="psum", bufs=1))

        def load_list(src, name):
            tile = keep.tile([P, S // 16], U16, name=name)
            nc.sync.dma_start(tile[:], src)
            return tile

        def load_words(src, width, name):
            tile = keep.tile([P, width], U32, name=name, tag=name, align_bytes=64)
            nc.sync.dma_start(tile[:].bitcast(I32), src[0].rearrange("p n t -> p (n t)").bitcast(I32))
            return tile

        def load_scale_rows(tile, src, row0, quadrants):
            for q in quadrants:
                rows = tile[32 * q + row0 : 32 * q + row0 + 4, :]
                nc.sync.dma_start(rows.bitcast(I32), src[0, 4 * q : 4 * q + 4, :].bitcast(I32))

        def deal(src, dtype, run, name):
            tile = keep.tile([P, S], dtype, name=name, tag=name, align_bytes=64)
            nc.vector.tensor_copy(
                tile[:].rearrange("p (t m i) -> p m t i", t=4, i=run),
                src[:].rearrange("p (m i t) -> p m t i", t=4, i=run),
            )
            return tile

        def pick(lst, name):
            words = keep.tile([P, S], U32, name=name + "_w", align_bytes=64)
            scales = keep.tile([P, S], U8, name=name + "_s", align_bytes=64)
            nc.vector.tensor_copy(words[:], xw[:].indirect(lst[:]))
            nc.vector.tensor_copy(scales[:], xs[:].indirect(lst[:]))
            return words, scales

        xs = keep.tile([P, T], U8, name="xs", align_bytes=64)
        ws = keep.tile([P, S], U8, name="ws", tag="ws", align_bytes=64)
        nc.vector.memset(ws[:].bitcast(I32), 0)
        quarter = keep.tile([P, 1], F32, name="quarter")
        warm = keep.tile([P, 1], F32, name="warm")
        nc.vector.memset(quarter[:], 0.25)
        floors = [keep.tile([P, 1], F32, name=f"floor{b}", tag=f"floor{b}", align_bytes=64) for b in range(2)]
        for floor in floors:
            nc.vector.memset(floor[:], 0.25)
        nc.scalar.activation(warm[:], quarter[:], ACT.Abs_reciprocal_sqrt, bias=quarter[:])

        for q in range(4):
            rows = x_scales[0, 4 * q : 4 * q + 4, :].bitcast(I32)
            nc.sync.dma_start(xs[32 * q : 32 * q + 32, :].bitcast(I32), rows.partition_broadcast(8))
        l_offs = load_list(offs, "l_offs")
        l_two = load_list(two, "l_two")
        l_cand = load_list(cand, "l_cand")
        xw = load_words(x_words, T, "xw")
        w1w = load_words(w1_words, S, "w1w")
        w2w = load_words(w2_words, S, "w2w")
        load_scale_rows(ws, w1_scales, 0, range(4))
        load_scale_rows(ws, w2_scales, 4, range(4))
        l1 = load_list(n1, "l1")
        l3 = load_list(n3, "l3")
        l2 = load_list(n2, "l2")
        l4 = load_list(n4, "l4")
        gain = keep.tile([P, 4], F32, name="gain")
        nc.sync.dma_start(gain[:], gs.rearrange("(p t) o -> p (t o)", t=4))
        l5 = load_list(n5, "l5")
        l6 = load_list(n6, "l6")

        banks = [psum.tile([P, S], F32, name=f"bank{b}") for b in range(8)]
        ident = keep.tile([P, P], F32, name="ident")
        make_identity(nc, ident[:])

        xo_w, xo_s = pick(l_offs, "xo")
        w1wd = deal(w1w, U32, 4, "w1wd")
        wsd = deal(ws, U8, 16, "wsd")
        w2wd = deal(w2w, U32, 4, "w2wd")
        later = keep.tile([P, 2 * S], U32, name="later", tag="ws", align_bytes=64)
        xt_w, xc_wd = later[:, :S], later[:, S:]
        xt_s = keep.tile([P, S], U8, name="xt_s", align_bytes=64)
        nc.vector.tensor_copy(xt_w, xw[:].indirect(l_two[:]))
        nc.vector.tensor_copy(xt_s[:], xs[:].indirect(l_two[:]))

        def project(ww, row0, xw_, xs_, bank0, name):
            rows = []
            for t in range(4):
                cols = slice(P * t, P * (t + 1))
                nc.tensor.matmul_mx(
                    out=banks[bank0 + t][:], lhsT=ww[:, cols].bitcast(FP8X4), lhsT_scale=wsd[row0:P, cols],
                    rhs=xw_[:].bitcast(FP8X4), rhs_scale=xs_[:], start=True, stop=True,
                )
                row = keep.tile([P, 2 * S if t < 2 else S], F32, name=f"{name}{t}")
                if t < 2:
                    (nc.vector if name == "y" else nc.gpsimd).memset(row[:, S:], 0.0)
                rows.append(row)
            return rows

        y = project(w1wd, 0, xo_w, xo_s, 0, "y")
        d = project(w2wd, 4, xt_w, xt_s, 4, "d")
        for pair in ((0, 1), (2, 3)):
            for t in pair:
                nc.scalar.copy(y[t][:, :S], banks[t][:])
            for t in pair:
                nc.scalar.copy(d[t][:, :S], banks[4 + t][:])

        xc_s = keep.tile([P, S], U8, name="xc_s", align_bytes=64)
        nc.vector.tensor_copy(xc_wd[:].rearrange("p (t m) -> p m t", t=4), xw[:].indirect(l_cand[:]))
        nc.vector.tensor_copy(xc_s[:], xs[:].indirect(l_cand[:]))
        xc_sd = deal(xc_s, U8, 16, "xc_sd")

        def turn(bank, part, ts, start, stop):
            for k, t in enumerate(ts):
                nc.tensor.matmul(
                    bank[:, P * k : P * (k + 1)], lhsT=part[:, t, :], rhs=ident[:], is_transpose=True,
                    start=(start and k == 0), stop=(stop and k == len(ts) - 1),
                )

        def quad(name, dtype=F32, n=BLK, tag=None, rows=4):
            return keep.tile([P, rows, n], dtype, name=name, tag=tag or name, align_bytes=64)

        def flat(tile):
            return tile[:].rearrange("p t n -> p (t n)")

        def weave(engine_copy, src, name, n=BLK, tag=None):
            dst = keep.tile([P, n, 4], BF16, name=name, tag=tag or name, align_bytes=64)
            engine_copy(dst[:].rearrange("p (c i) t -> p c t i", i=4), src.rearrange("p t (c i) -> p c t i", i=4))
            return dst

        zq = keep.tile([P, S], U32, name="zq", align_bytes=64)
        zs = keep.tile([P, S], U8, name="zs", tag="zs", align_bytes=64)
        w = [keep.tile([P, S], F32, name=f"w{t}") for t in range(4)]
        s3 = {}
        last = S // BLK - 1

        zp_a, zp_b = quad("zp_a", BF16, n=256), quad("zp_b", BF16)
        end = quad("end")

        def z_wide():
            ya, first, yb, gap = (quad(name, n=S, rows=2) for name in ("ya", "first", "yb", "gap"))
            for t in range(2):
                nc.vector.tensor_copy(ya[:, t, :], y[t][:].indirect(l1[:]))
            for t in range(2):
                nc.vector.tensor_tensor(first[:, t, :], d[t][:].indirect(l3[:]), ya[:, t, :], ALU.add)
            for t in range(2):
                nc.vector.tensor_tensor(yb[:, t, :], y[t][:].indirect(l2[:]), first[:, t, :], ALU.subtract)
            for t in range(2):
                nc.vector.tensor_tensor(gap[:, t, :], d[t][:].indirect(l4[:]), yb[:, t, :], ALU.add)
            for t in range(2):
                rise, turned = quad(f"rise{t}"), quad(f"turned{t}")
                across, back = banks[t], banks[2 + t]
                turn(across, first[:, t, :].rearrange("p (b j) -> p b j", b=4), range(4), True, False)
                nc.scalar.activation(flat(rise), gap[:, t, :], ACT.Relu)
                turn(across, rise, range(4), False, True)
                nc.scalar.copy(flat(turned), across[:])
                turn(back, turned, range(4), True, True)
                nc.scalar.activation(zp_a[:, t, :], back[:, :256], ACT.Copy, scale=gain[:, t : t + 1])
                nc.scalar.activation(zp_b[:, t, :], back[:, 256:384], ACT.Copy, scale=gain[:, t : t + 1])
                nc.scalar.copy(end[:, t, :], back[:, S - BLK :])

        def fetch_y(out, k, j0):
            n = out.shape[1]
            nc.vector.tensor_copy(out, y[2 + k % 2][:].indirect((l1, l2)[k // 2][:, j0 // 16 : (j0 + n) // 16]))

        def add_d(out, other, k, j0):
            n = out.shape[1]
            window = d[2 + k % 2][:].indirect((l3, l4)[k // 2][:, j0 // 16 : (j0 + n) // 16])
            nc.vector.tensor_tensor(out, window, other, ALU.add)

        def scale_plane(planes, t, big):
            nc.scalar.activation(planes[:, t, :], big, ACT.Copy, scale=gain[:, t : t + 1])

        def row(name, n, tag=None):
            return keep.tile([P, n], F32, name=name, tag=tag or name, align_bytes=64)

        def score_bank(b, t):
            return banks[(3, 2, 1, 7)[t]] if b == last else banks[4 + b]

        def z_score(zi, j0, n):
            nc.vector.quantize_mx(
                out=zq[:, j0 : j0 + n].bitcast(FP8X4), scales=zs[:, j0 : j0 + n], in_=zi[:].rearrange("p n t -> p (n t)")
            )
            for b in range(j0 // BLK, (j0 + n) // BLK):
                cs = slice(b * BLK, (b + 1) * BLK)
                for t in range(4):
                    cols = slice(P * t, P * (t + 1))
                    nc.tensor.matmul_mx(
                        out=score_bank(b, t)[:, cols], lhsT=xc_wd[:, cols].bitcast(FP8X4), lhsT_scale=xc_sd[:, cols],
                        rhs=zq[:, cs].bitcast(FP8X4), rhs_scale=zs[:, cs], start=True, stop=True,
                    )
                for t in range(4):
                    nc.scalar.activation(
                        w[t][:, cs], score_bank(b, t)[:, P * t : P * (t + 1)], ACT.Copy, scale=-0.3125 * 0.0625
                    )

        def own_term(b, tile):
            s3[b] = tile
            for lo, hi in ((0, 1), (1, 2), (2, 3), (3, 4)) if b == last else ((0, 4),):
                nc.scalar.activation(
                    flat(s3[b])[:, P * lo : P * hi], score_bank(b, lo)[:, P * lo : P * hi], ACT.Copy,
                    scale=0.3125 * 0.0625 * 5.0 / 3.0,
                )

        z_wide()
        ys = [row(f"yA{k}", 256, tag) for k, tag in enumerate(("ya", "yb", "first", "gap"))]
        late = row("late", 256 + 4 * BLK, "turned1")
        sums = [row("dA0", 256)[:], row("dA1", 256, "turned0")[:], row("dA2", 256)[:], late[:, :256]]
        for t in range(2):
            for k in (t, 2 + t):
                fetch_y(ys[k][:], k, 0)
            for k in (t, 2 + t):
                add_d(sums[k], ys[k][:], k, 0)
            big = row(f"bigA{t}", 256, "rise1" if t == 0 else None)
            nc.vector.tensor_tensor(big[:], sums[t], sums[2 + t], ALU.max)
            scale_plane(zp_a, 2 + t, big[:])
        zi_a = weave(nc.scalar.copy, zp_a[:], "ziA", 256)

        sums, big = quad("dB"), quad("bigB", rows=2)
        for k in range(4):
            fetch_y(late[:, 256 + BLK * k : 256 + BLK * (k + 1)], k, 256)
        for k in range(4):
            add_d(sums[:, k, :], late[:, 256 + BLK * k : 256 + BLK * (k + 1)], k, 256)
        nc.vector.tensor_tensor(big[:], sums[:, 0:2, :], sums[:, 2:4, :], ALU.max)
        for t in range(2):
            scale_plane(zp_b, 2 + t, big[:, t, :])
        zi_b = weave(nc.scalar.copy, zp_b[:], "ziB")
        z_score(zi_a, 0, 256)

        ys, sums = quad("yC", tag="zp_a"), [quad("dC0", rows=2)]
        for k in range(4):
            fetch_y(ys[:, k, :], k, 384)
        for k in range(2):
            add_d(sums[0][:, k, :], ys[:, k, :], k, 384)
        z_score(zi_b, 256, BLK)
        sums.append(quad("dC1", rows=2, tag="zp_b"))
        for k in range(2, 4):
            add_d(sums[1][:, k - 2, :], ys[:, k, :], k, 384)
        nc.vector.tensor_tensor(end[:, 2:4, :], sums[0][:], sums[1][:], ALU.max)
        zi_c = keep.tile([P, BLK, 4], BF16, name="ziC", align_bytes=64)
        nc.vector.tensor_tensor(
            zi_c[:].rearrange("p (c i) t -> p c t i", i=4), end[:].rearrange("p t (c i) -> p c t i", i=4),
            gain[:].unsqueeze(1).unsqueeze(3).to_broadcast([P, BLK // 4, 4, 4]), ALU.mult,
        )
        z_score(zi_c, 384, BLK)
        for b, tag in ((0, None), (3, "zs"), (1, "xc_sd"), (2, "ws")):
            own_term(b, quad(f"s3_{b}", tag=tag))

        oq = keep.tile([P, S], U32, name="oq", align_bytes=64)
        os_ = keep.tile([P, S], U8, name="os_", align_bytes=64)
        out_rows = out_0.rearrange("(p t) j -> p t j", t=4)
        out_codes = out_1[0].rearrange("p n t -> p (n t)").bitcast(I32)
        res = [quad(f"res{b}") for b in range(4)]

        def first_places(name, j0, after):
            ga = quad(name, n=2 * BLK, tag=after)
            for t in range(4):
                nc.vector.tensor_copy(ga[:, t, :], w[t][:].indirect(l5[:, j0 // 16 : (j0 + 2 * BLK) // 16]))
            return ga[:, :, :BLK], ga[:, :, BLK:]

        def doubled(name, ga, after):
            neg = quad(name, tag=after, rows=ga.shape[1])
            nc.scalar.activation(neg[:], ga, ACT.Copy, scale=-2.0)
            return neg[:]

        def both_places(b, ga, after):
            u = quad(f"u{b}", tag=after)
            for t in range(4):
                window = w[t][:].indirect(l6[:, b * BLK // 16 : (b + 1) * BLK // 16])
                nc.vector.tensor_tensor(u[:, t, :], window, ga[:, t, :], ALU.add)
            return u[:]

        def o_front(name, b, ts, neg, u, lin, diff, num_after=None):
            m = len(ts)
            own = range(m)
            num, sq_d, sq_l = quad(f"num{name}", rows=m, tag=num_after), quad(f"sq_d{name}", rows=m), quad(f"sq_l{name}", rows=m)
            turn(lin, s3[b], ts, True, False)
            turn(diff, neg, own, True, False)
            turn(lin, u, own, False, True)
            nc.scalar.activation(flat(sq_l), lin[:, : m * P], ACT.Square, scale=1.2 * ROOT_HALF)
            turn(diff, u, own, False, True)
            nc.scalar.activation(flat(sq_d), diff[:, : m * P], ACT.Square, scale=3.2 * ROOT_HALF)
            nc.vector.scalar_tensor_tensor(num[:], s3[b][:, ts[0] : ts[0] + m, :], 1.32, u, ALU.mult, ALU.add)
            return name, b, ts, sq_d, sq_l, num

        def o_sum(name, b, ts, sq_d, sq_l, num, bank):
            m = len(ts)
            r = quad(f"r{name}", rows=m)
            turn(bank, sq_l, range(m), True, False)
            turn(bank, sq_d, range(m), False, True)
            nc.scalar.activation(flat(r), bank[:, : m * P], ACT.Abs_reciprocal_sqrt, bias=(floors + [quarter])[b][:])
            return b, ts, num, r

        def o_front_direct(name, ts, ga, u, after):
            own = s3[last][:, ts[0] : ts[0] + 2, :]
            lin, diff = after[:, 0:2, :], after[:, 2:4, :]
            num, sq_d, sq_l = quad(f"num{name}", rows=2), quad(f"sq_d{name}", rows=2), quad(f"sq_l{name}", rows=2)
            nc.vector.tensor_tensor(lin[:], u, own, ALU.add)
            nc.scalar.activation(sq_l[:], lin[:], ACT.Square, scale=1.2 * ROOT_HALF)
            nc.vector.scalar_tensor_tensor(diff[:], ga, -2.0, u, ALU.mult, ALU.add)
            nc.scalar.activation(sq_d[:], diff[:], ACT.Square, scale=3.2 * ROOT_HALF)
            nc.vector.scalar_tensor_tensor(num[:], own, 1.32, u, ALU.mult, ALU.add)
            return name, ts, sq_d, sq_l, num

        def o_sum_direct(name, ts, sq_d, sq_l, num):
            q, r = quad(f"q{name}", rows=2), quad(f"r{name}", rows=2)
            nc.vector.tensor_tensor(q[:], sq_l[:], sq_d[:], ALU.add)
            nc.scalar.activation(r[:], q[:], ACT.Abs_reciprocal_sqrt, bias=quarter[:])
            return last, ts, num, r

        def o_final(b, ts, num, r):
            rows = slice(ts[0], ts[0] + len(ts))
            nc.vector.tensor_tensor(res[b][:, rows, :], num[:], r[:], ALU.mult)
            nc.sync.dma_start(out_rows[:, rows, b * BLK : (b + 1) * BLK], res[b][:, rows, :])

        def o_weave(b, after=None):
            return weave(nc.vector.tensor_copy if b >= last - 1 else nc.scalar.copy, res[b][:], f"ri{b}", tag=after)

        def o_planes(b, ri):
            cs = slice(b * BLK, (b + 1) * BLK)
            nc.vector.quantize_mx(out=oq[:, cs].bitcast(FP8X4), scales=os_[:, cs], in_=ri[:].rearrange("p n t -> p (n t)"))
            nc.sync.dma_start(out_codes[:, cs], oq[:, cs].bitcast(I32))

        whole = [0, 1, 2, 3]
        ga0, ga1 = first_places("ga01", 0, None)
        neg0, neg1 = doubled("neg0", ga0, None), doubled("neg1", ga1, None)
        f0 = o_front("0", 0, whole, neg0, both_places(0, ga0, None), banks[0], banks[1])
        s0 = o_sum(*f0, banks[2])
        f1 = o_front("1", 1, whole, neg1, both_places(1, ga1, None), banks[1], banks[0])
        ga2, ga3 = first_places("ga23", 256, "neg0")
        o_final(*s0)
        s1 = o_sum(*f1, banks[4])
        r0 = o_weave(0, "sq_l1")
        f2 = o_front("2", 2, whole, doubled("neg2", ga2, "u1"), both_places(2, ga2, "floor0"), banks[0], banks[1])
        o_planes(0, r0)
        o_final(*s1)
        s2 = o_sum(*f2, banks[2])
        r1 = o_weave(1, "sq_l2")
        u = both_places(3, ga3, "floor1")
        forms = quad("forms", rows=8, tag="sq_d2")
        f3a = o_front_direct("3a", [0, 1], ga3[:, 0:2, :], u[:, 0:2, :], forms[:, 0:4, :])
        f3b = o_front_direct("3b", [2, 3], ga3[:, 2:4, :], u[:, 2:4, :], forms[:, 4:8, :])
        o_planes(1, r1)
        o_final(*s2)
        s3a = o_sum_direct(*f3a)
        s3b = o_sum_direct(*f3b)
        r2 = o_weave(2)
        o_final(*s3a)
        o_final(*s3b)
        o_planes(2, r2)
        o_planes(3, o_weave(3))
        for q in range(4):
            queue = nc.sync if q % 2 == 0 else nc.scalar
            queue.dma_start(out_2[0, 4 * q : 4 * q + 4, :].bitcast(I32), os_[32 * q : 32 * q + 4, :].bitcast(I32))
